import numpy as np
import ml_dtypes


def mxq(x, axis, fmt="e4m3"):
    dtype, down = {"e4m3": (ml_dtypes.float8_e4m3fn, 7), "e5m2": (ml_dtypes.float8_e5m2, 14)}[fmt]
    v = np.moveaxis(np.asarray(x, np.float32).astype(ml_dtypes.bfloat16).astype(np.float64), axis, -1)
    blocks = v.reshape(v.shape[:-1] + (-1, 32))
    amax = np.abs(blocks).max(-1, keepdims=True)
    byte = np.maximum(np.where(amax > 0, np.frexp(amax)[1] - 1 + 127, 0) - down, 1)
    scale = np.exp2(byte - 127.0)
    codes = (blocks / scale).astype(np.float32).astype(dtype).astype(np.float64)
    return np.moveaxis((codes * scale).reshape(v.shape), -1, axis)


WIDE = False


def mx_kscale(k):
    if not WIDE:
        return np.ones(k)
    levels = np.array([30, -30])
    if k % 512:
        return np.exp2(np.random.permutation(np.resize(levels, k // 32))).repeat(32)
    a = np.empty((k // 512, 16))
    for p in range(k // 512):
        a[p, :8] = np.random.permutation(np.resize(levels, 8))
        for g in range(8):
            far = levels[np.abs(levels - a[p, g]) >= 10]
            a[p, g + 8] = far[np.random.randint(len(far))]
    return np.exp2(a.ravel()).repeat(32)


def f64(x):
    return np.asarray(x).astype(np.float64)


def striped(idx):
    return np.tile(np.asarray(idx).reshape(-1, 16).T, (8, 1)).astype(np.uint16)


def unstriped(offs):
    return offs[:16].T.reshape(-1).astype(np.int64)


E2M1 = np.array([0.0, 0.5, 1.0, 1.5, 2.0, 3.0, 4.0, 6.0, -0.0, -0.5, -1.0, -1.5, -2.0, -3.0, -4.0, -6.0])


def pack_weight(w, fmt):
    k, n = w.shape
    w = f64(np.asarray(w, np.float32).astype(ml_dtypes.bfloat16)).reshape(k // 32, 32, n)
    amax = np.abs(w).max(1)
    if fmt == "e4m3":
        byte = np.frexp(amax)[1] - 1 + 127 - 7
    else:
        mant, ex = np.frexp(amax / 6.0)
        byte = np.where(mant > 0.5, ex, ex - 1) + 127
    byte = np.clip(np.where(amax > 0, byte, 1), 1, 254)
    scaled = (w * np.exp2(127.0 - byte)[:, None, :]).reshape(k, n).astype(np.float32)
    by_word = np.ascontiguousarray(scaled.reshape(k // 512, 128, 4, n).transpose(0, 1, 3, 2))
    if fmt == "e4m3":
        words = by_word.astype(ml_dtypes.float8_e4m3fn).view(np.uint8)
    else:
        c = by_word.astype(ml_dtypes.float4_e2m1fn).view(np.uint8) & 0xF
        words = (c[..., 0::2] | (c[..., 1::2] << 4)).reshape(k // 512, 128, 2 * n)
    return np.ascontiguousarray(words), np.ascontiguousarray(byte.astype(np.uint8).reshape(k // 512, 16, n))


def unpack_weight(words, scales, fmt):
    g, _, n = scales.shape
    words = np.ascontiguousarray(words).reshape(g, 128, n, -1)
    if fmt == "e4m3":
        vals = words.view(ml_dtypes.float8_e4m3fn).astype(np.float64)
    else:
        nib = np.empty((g, 128, n, 4), np.uint8)
        nib[..., 0::2] = words & 0xF
        nib[..., 1::2] = words >> 4
        vals = E2M1[nib]
    vals = vals * np.repeat(np.exp2(scales.astype(np.float64) - 127.0), 8, axis=1)[..., None]
    return vals.transpose(0, 1, 3, 2).reshape(g * 512, n)


def bf(x):
    return np.asarray(x, np.float32).astype(ml_dtypes.bfloat16)


def planes(Y):
    r, m = Y.shape
    b = f64(bf(Y)).reshape(r // 32, 32, m)
    amax = np.abs(b).max(1)
    byte = np.clip(np.where(amax > 0, np.frexp(amax)[1] - 1 + 127 - 7, 1), 1, 254)
    codes = (b * np.exp2(127.0 - byte)[:, None, :]).reshape(r, m).astype(np.float32).astype(ml_dtypes.float8_e4m3fn).view(np.uint8)
    words = codes.reshape(r // 512, 128, 4, m).transpose(0, 1, 3, 2)
    return np.ascontiguousarray(words), np.ascontiguousarray(byte.astype(np.uint8).reshape(r // 512, 16, m))


N, M, K, T, J = 1024, 512, 512, 1024, 512


def setup_inputs():
    n = np.random.standard_normal
    idx = np.random.permutation(T)[:J]
    idx2 = np.random.permutation(T)[:J]
    fn = mx_kscale(N)
    fm = mx_kscale(M)
    gp = pack_weight(n((N, J)) / fn[:, None], "e2m1")
    wup = pack_weight(n((N, M)) * 1 / np.sqrt(N) * fn[:, None] * fm, "e4m3")
    wlp = pack_weight(n((M, K)) * 1 / np.sqrt(M) / fm[:, None], "e2m1")
    return {
        "g_words": gp[0],
        "g_scales": gp[1],
        "wu_words": wup[0],
        "wu_scales": wup[1],
        "gt": (n((M, T)) * fm[:, None]).astype(np.float32),
        "wl_words": wlp[0],
        "wl_scales": wlp[1],
        "offs": striped(idx),
        "offs2": striped(idx2),
    }


def reference(g_words, g_scales, wu_words, wu_scales, gt, wl_words, wl_scales, offs, offs2):
    idx = unstriped(offs)
    idx2 = unstriped(offs2)
    gu = unpack_weight(g_words, g_scales, "e2m1")
    wuu = unpack_weight(wu_words, wu_scales, "e4m3")
    wlu = unpack_weight(wl_words, wl_scales, "e2m1")
    d = wuu.T @ gu
    pa = np.zeros((M, T))
    pa[:, idx] = d
    pb = np.zeros((M, T))
    pb[:, idx2] = d
    s = 0.5 * (pa + pb) + f64(gt)
    sq = mxq(s, 0, "e5m2")
    y = wlu.T @ sq
    words, scales = planes(y)
    return y, words, scales

@@ -1,0 +1,277 @@
+from contextlib import ExitStack
+
+import concourse.mybir as mybir
+from concourse.masks import make_identity
+
+N, M, K, T, J = 1024, 512, 512, 1024, 512
+FLOPS = 2 * N * M * J + 2 * M * K * T
+
+F32 = mybir.dt.float32
+BF16 = mybir.dt.bfloat16
+I32 = mybir.dt.int32
+U32 = mybir.dt.uint32
+U16 = mybir.dt.uint16
+U8 = mybir.dt.uint8
+E4M3X4 = mybir.dt.float8_e4m3fn_x4
+E5M2X4 = mybir.dt.float8_e5m2_x4
+E2M1X4 = mybir.dt.float4_e2m1fn_x4
+COPY = mybir.ActivationFunctionType.Copy
+ADD = mybir.AluOpType.add
+
+P = 128
+R = 4
+HALF = 512
+FIRST = 128
+
+
+def tile_list_merged_gradient_back_pl_kernel(
+    tc, g_words, g_scales, wu_words, wu_scales, gt, wl_words, wl_scales, offs, offs2, out_0, out_1, out_2
+):
+    nc = tc.nc
+    with ExitStack() as ctx:
+        sb = ctx.enter_context(tc.tile_pool(name="sb", bufs=1))
+        ps = ctx.enter_context(tc.psum_pool(name="ps", bufs=1))
+
+        def bank(b, shape, name):
+            return ps.tile(shape, F32, name=name, tag="bank%d" % b)
+
+        def sbt(shape, dtype, name):
+            return sb.tile(shape, dtype, name=name, align_bytes=64)
+
+        list_a = sb.tile([P, J // 16], U16, name="list_a")
+        list_b = sb.tile([P, J // 16], U16, name="list_b")
+        scales_in = sbt([P, 5, HALF], U8, "scales_in")
+        wu_raw = sb.tile([P, 2, M], U32, name="wu_raw", tag="stage", align_bytes=64)
+        g_sb = sbt([P, 2, 2 * J], U8, "g_sb")
+        wl_raw = sbt([P, 2 * K], U8, "wl_raw")
+        page_a = sbt([P, T], F32, "page_a")
+        page_b = sbt([P, T], F32, "page_b")
+        ident = sbt([P, P], F32, "ident")
+
+        nc.gpsimd.memset(scales_in[:].rearrange("p a c -> p (a c)").bitcast(I32), 0)
+        nc.vector.memset(page_a[:], 0.0)
+        nc.vector.memset(page_b[:], 0.0)
+
+        def load_scale_rows(queue, q, rows, src):
+            queue.dma_start(
+                out=scales_in[32 * q : 32 * q + 4, rows, :].bitcast(I32),
+                in_=src[:, 4 * q : 4 * q + 4, :].rearrange("z q c -> q z c").bitcast(I32),
+            )
+
+        nc.sync.dma_start(list_a[:], offs)
+        nc.sync.dma_start(out=g_sb[:].bitcast(I32), in_=g_words.rearrange("z p c -> p z c").bitcast(I32))
+        nc.sync.dma_start(list_b[:], offs2)
+        nc.sync.dma_start(out=wu_raw[:].bitcast(I32), in_=wu_words.rearrange("z p c r -> p z (c r)").bitcast(I32))
+        for q in range(4):
+            load_scale_rows(nc.sync if q < 2 else nc.scalar, q, slice(2, 4), wu_scales)
+        for q in range(4):
+            load_scale_rows((nc.sync, nc.scalar, nc.sync, nc.gpsimd)[q], q, slice(0, 2), g_scales)
+        nc.gpsimd.dma_start(out=wl_raw[:].bitcast(I32), in_=wl_words[0].bitcast(I32))
+        make_identity(nc, ident[:])
+        for q in range(4):
+            load_scale_rows(nc.sync, q, slice(4, 5), wl_scales)
+        gt_rows = gt.rearrange("(p r) t -> p r t", r=R)
+
+        def load_gt(r):
+            tile = sb.tile([P, T], F32, name="gt%d" % r, tag="stage", align_bytes=64)
+            nc.sync.dma_start(out=tile[:], in_=gt_rows[:, r, :])
+            return tile
+
+        wu_sb = sbt([P, 2, R, P], U32, "wu_sb")
+        wu_sc = sbt([P, 2, R, P], U8, "wu_sc")
+
+        def deal_wu(r0, r1):
+            nc.vector.tensor_copy(
+                out=wu_sc[:, :, r0:r1, :].rearrange("p z r q -> p z q r"),
+                in_=scales_in[:, 2:4, :].rearrange("p z (q r) -> p z q r", r=R)[:, :, :, r0:r1],
+            )
+            nc.vector.tensor_copy(
+                out=wu_sb[:, :, r0:r1, :].bitcast(I32).rearrange("p z r q -> p z q r"),
+                in_=wu_raw[:].bitcast(I32).rearrange("p z (q r) -> p z q r", r=R)[:, :, :, r0:r1],
+            )
+
+        deal_wu(0, 1)
+
+        def first_product(acc, r, j0, width):
+            for z in range(2):
+                nc.tensor.matmul_mx(
+                    out=acc,
+                    lhsT=wu_sb[:, z, r, :].bitcast(E4M3X4),
+                    lhsT_scale=wu_sc[:, z, r, :],
+                    rhs=g_sb[:, z, 2 * j0 : 2 * (j0 + width)].bitcast(E2M1X4),
+                    rhs_scale=scales_in[:, z, j0 : j0 + width],
+                    start=(z == 0),
+                    stop=(z == 1),
+                )
+
+        pieces = [(0, 0, FIRST), (0, FIRST, J), (1, 0, J), (2, 0, J), (3, 0, J)]
+        d_sb = {}
+
+        def make_d(i):
+            r, j0, j1 = pieces[i]
+            acc = bank(i, [P, j1 - j0], "d_ps%d" % i)
+            step = HALF if j1 - j0 == HALF else P
+            for j in range(j0, j1, step):
+                first_product(acc[:, j - j0 : j - j0 + step], r, j, step)
+            d_sb[i] = sbt([P, j1 - j0], F32, "d%d" % i)
+            nc.scalar.activation(d_sb[i][:], acc[:], COPY, scale=0.5)
+
+        def scatter(page, lst, i):
+            r, j0, j1 = pieces[i]
+            nc.vector.tensor_copy(page[:].indirect(lst[:, j0 // 16 : j1 // 16]), d_sb[i][:])
+
+        make_d(0)
+        make_d(1)
+        scatter(page_a, list_a, 0)
+        scatter(page_b, list_b, 0)
+        deal_wu(1, R)
+        for i in range(2, len(pieces)):
+            make_d(i)
+
+        def turn_add(acc, src, t0, start, stop):
+            blocks = acc.shape[1]
+            for tb in range(blocks):
+                c0 = t0 + tb * P
+                nc.tensor.matmul(
+                    acc[:, tb, :], lhsT=src[:, c0 : c0 + P], rhs=ident[:], is_transpose=True,
+                    start=(start and tb == 0), stop=(stop and tb == blocks - 1),
+                )
+
+        wl_sb = sbt([P, R, 2 * P], U8, "wl_sb")
+        wl_sc = sbt([P, R, P], U8, "wl_sc")
+
+        pairs = [[sbt([P, 4, P, 2], BF16, "pairs%d%d" % (h, u)) for u in range(2)] for h in range(2)]
+        s_bf = [sbt([P, HALF, R], BF16, "s_bf%d" % h) for h in range(2)]
+        back = [[bank(1 + 2 * h + q, [P, 2, 256], "back%d%d" % (h, q)) for q in range(2)] for h in range(2)]
+
+        def turn_back(h, u):
+            words = pairs[h][u][:].rearrange("t b p e -> t b (p e)").bitcast(F32)
+            for tb in range(4):
+                c0 = (tb % 2) * P
+                nc.tensor.transpose(back[h][tb // 2][:, u, c0 : c0 + P], words[:, tb, :], ident[:])
+
+        def weave(h):
+            words = s_bf[h][:].rearrange("p t r -> p (t r)").bitcast(F32).rearrange("p (t u) -> p t u", u=2)
+            for q in range(2):
+                nc.scalar.copy(words[:, 256 * q : 256 * (q + 1), :], back[h][q][:].rearrange("p u t -> p t u"))
+
+        gt_sb = {}
+        for r in range(3):
+            gt_sb[r] = load_gt(r)
+            sums = [bank(5 + h, [P, 4, P], "sum%d%d" % (r, h)) for h in range(2)]
+            scatter(page_a, list_a, r + 1)
+            scatter(page_b, list_b, r + 1)
+            if r == 0:
+                nc.vector.tensor_copy(
+                    out=wl_sb[:].bitcast(U16).rearrange("p r q -> p q r"),
+                    in_=wl_raw[:].bitcast(U16).rearrange("p (q r) -> p q r", r=R),
+                )
+                nc.vector.tensor_copy(
+                    out=wl_sc[:].rearrange("p r q -> p q r"),
+                    in_=scales_in[:, 4, :].rearrange("p (q r) -> p q r", r=R),
+                )
+            for h in range(2):
+                turn_add(sums[h], page_a, h * HALF, True, False)
+            for h in range(2):
+                turn_add(sums[h], gt_sb[r], h * HALF, False, False)
+            for h in range(2):
+                turn_add(sums[h], page_b, h * HALF, False, True)
+            for h in range(2):
+                if r == 2 and h == 0:
+                    nc.scalar.copy(pairs[0][1][:], sums[0][:].unsqueeze(3).to_broadcast([P, 4, P, 2]))
+                else:
+                    nc.scalar.copy(pairs[h][r // 2][:, :, :, r % 2], sums[h][:])
+            if r == 1:
+                turn_back(0, 0)
+                turn_back(1, 0)
+        turn_back(0, 1)
+        weave(0)
+
+        gt_sb[3] = load_gt(3)
+        scatter(page_a, list_a, 4)
+        part = bank(5, [P, 4, P], "part")
+        turn_add(part, gt_sb[3], 0, True, False)
+        turn_add(part, page_a, 0, False, True)
+        part_sb = sbt([P, 4, P], F32, "part_sb")
+        nc.scalar.copy(part_sb[:], part[:])
+        part_back = bank(6, [P, HALF], "part_back")
+        for tb in range(4):
+            nc.tensor.transpose(part_back[:, tb * P : (tb + 1) * P], part_sb[:, tb, :], ident[:])
+        last = [bank((5, 7)[q], [P, 2, P], "last%d" % q) for q in range(2)]
+        for q in range(2):
+            turn_add(last[q], gt_sb[3], HALF + 256 * q, True, False)
+            turn_add(last[q], page_a, HALF + 256 * q, False, False)
+        scatter(page_b, list_b, 4)
+        for q in range(2):
+            turn_add(last[q], page_b, HALF + 256 * q, False, True)
+
+        s_words = [sbt([P, HALF], U32, "s_words%d" % h) for h in range(2)]
+        s_sc = [sbt([P, HALF], U8, "s_sc%d" % h) for h in range(2)]
+        for q in range(2):
+            cols = slice(256 * q, 256 * (q + 1))
+            nc.vector.tensor_tensor(s_bf[0][:, cols, 3], part_back[:, cols], page_b[:, cols], ADD)
+        for q in range(2):
+            cols = slice(256 * q, 256 * (q + 1))
+            nc.vector.quantize_mx(
+                out=s_words[0][:, cols].bitcast(E5M2X4), scales=s_sc[0][:, cols],
+                in_=s_bf[0][:, cols, :].rearrange("p t r -> p (t r)"),
+            )
+        for q in range(2):
+            nc.scalar.copy(pairs[1][1][:, 2 * q : 2 * q + 2, :, 1], last[q][:])
+        turn_back(1, 1)
+        weave(1)
+
+        y_rows = out_0.rearrange("(p r) t -> p r t", r=R)
+        y_sb = [sbt([P, R, HALF], F32, "y_sb%d" % h) for h in range(2)]
+        y_bf = [sbt([P, HALF, R], BF16, "y_bf%d" % h) for h in range(2)]
+        y_words = sbt([P, T], U32, "y_words")
+        y_sc = sbt([P, T], U8, "y_sc")
+        y_banks = [[5, 7, 5, 7], [6, 0, 1, 2]]
+        words_out = out_1[0].rearrange("p t r -> p (t r)").bitcast(I32)
+
+        def second_product(h, r, on_vector):
+            acc = bank(y_banks[h][r], [P, HALF], "y%d%d" % (h, r))
+            nc.tensor.matmul_mx(
+                out=acc[:], lhsT=wl_sb[:, r, :].bitcast(E2M1X4), lhsT_scale=wl_sc[:, r, :],
+                rhs=s_words[h][:].bitcast(E5M2X4), rhs_scale=s_sc[h][:], start=True, stop=True,
+            )
+            if on_vector:
+                nc.vector.tensor_copy(y_sb[h][:, r, :], acc[:])
+            else:
+                nc.scalar.copy(y_sb[h][:, r, :], acc[:])
+            nc.sync.dma_start(out=y_rows[:, r, h * HALF : (h + 1) * HALF], in_=y_sb[h][:, r, :])
+
+        def planes(h, t0, t1):
+            nc.vector.tensor_copy(
+                out=y_bf[h][:, t0:t1, :].rearrange("p (c i) r -> p c r i", i=4),
+                in_=y_sb[h][:, :, t0:t1].rearrange("p r (c i) -> p c r i", i=4),
+            )
+
+        def planes_q(h, t0, t1):
+            cols = slice(h * HALF + t0, h * HALF + t1)
+            nc.vector.quantize_mx(
+                out=y_words[:, cols].bitcast(E4M3X4), scales=y_sc[:, cols],
+                in_=y_bf[h][:, t0:t1, :].rearrange("p t r -> p (t r)"),
+            )
+
+        second_product(0, 0, True)
+        second_product(0, 1, False)
+        nc.vector.quantize_mx(
+            out=s_words[1][:].bitcast(E5M2X4), scales=s_sc[1][:], in_=s_bf[1][:].rearrange("p t r -> p (t r)")
+        )
+        second_product(0, 2, True)
+        second_product(0, 3, False)
+        for r in range(R):
+            second_product(1, r, False)
+        for h in range(2):
+            planes(h, 0, 256)
+            planes(h, 256, 512)
+            for q in range(2):
+                planes_q(h, 256 * q, 256 * (q + 1))
+                cols = slice(h * HALF + 256 * q, h * HALF + 256 * (q + 1))
+                nc.sync.dma_start(out=words_out[:, cols], in_=y_words[:, cols].bitcast(I32))
+        for q in range(4):
+            queue = nc.sync if q % 2 == 0 else nc.scalar
+            queue.dma_start(
+                out=out_2[0, 4 * q : 4 * q + 4, :].bitcast(I32), in_=y_sc[32 * q : 32 * q + 4, :].bitcast(I32)
+            )

@@ -40,36 +40,43 @@ def tile_list_merged_gradient_back_pl_kernel(
 
         list_a = sb.tile([P, J // 16], U16, name="list_a")
         list_b = sb.tile([P, J // 16], U16, name="list_b")
-        scales_in = sbt([P, 5, HALF], U8, "scales_in")
+        wu_sc_raw = sbt([P, 2, M], U8, "wu_sc_raw")
+        g_sc = sbt([P, 2, J], U8, "g_sc")
+        wl_sc_raw = sbt([P, 1, K], U8, "wl_sc_raw")
         wu_raw = sb.tile([P, 2, M], U32, name="wu_raw", tag="stage", align_bytes=64)
-        g_sb = sbt([P, 2, 2 * J], U8, "g_sb")
+        g_first = sbt([P, 2, 2 * FIRST], U8, "g_first")
+        g_rest = sbt([P, 2, 2 * (J - FIRST)], U8, "g_rest")
         wl_raw = sbt([P, 2 * K], U8, "wl_raw")
         page_a = sbt([P, T], F32, "page_a")
         page_b = sbt([P, T], F32, "page_b")
         ident = sbt([P, P], F32, "ident")
 
-        nc.gpsimd.memset(scales_in[:].rearrange("p a c -> p (a c)").bitcast(I32), 0)
+        for plane in (wu_sc_raw, g_sc, wl_sc_raw):
+            nc.vector.memset(plane[:].rearrange("p a c -> p (a c)").bitcast(I32), 0)
         nc.vector.memset(page_a[:], 0.0)
         nc.vector.memset(page_b[:], 0.0)
+        nc.vector.memset(ident[:], 0.0)
+        make_identity(nc, ident[:], nomemset=True)
 
-        def load_scale_rows(queue, q, rows, src):
+        def load_scale_rows(queue, q, plane, src):
             queue.dma_start(
-                out=scales_in[32 * q : 32 * q + 4, rows, :].bitcast(I32),
+                out=plane[32 * q : 32 * q + 4].bitcast(I32),
                 in_=src[:, 4 * q : 4 * q + 4, :].rearrange("z q c -> q z c").bitcast(I32),
             )
 
-        nc.sync.dma_start(list_a[:], offs)
-        nc.sync.dma_start(out=g_sb[:].bitcast(I32), in_=g_words.rearrange("z p c -> p z c").bitcast(I32))
-        nc.sync.dma_start(list_b[:], offs2)
+        g_rows = g_words.rearrange("z p c -> p z c")
+        nc.sync.dma_start(out=g_first[:].bitcast(I32), in_=g_rows[:, :, 0 : 2 * FIRST].bitcast(I32))
+        for q in range(4):
+            load_scale_rows(nc.sync if q < 2 else nc.scalar, q, wu_sc_raw, wu_scales)
         nc.sync.dma_start(out=wu_raw[:].bitcast(I32), in_=wu_words.rearrange("z p c r -> p z (c r)").bitcast(I32))
         for q in range(4):
-            load_scale_rows(nc.sync if q < 2 else nc.scalar, q, slice(2, 4), wu_scales)
+            load_scale_rows(nc.sync if q < 1 else nc.scalar, q, g_sc, g_scales)
+        nc.sync.dma_start(list_a[:], offs)
+        nc.scalar.dma_start(out=g_rest[:].bitcast(I32), in_=g_rows[:, :, 2 * FIRST : 2 * J].bitcast(I32))
+        nc.sync.dma_start(out=wl_raw[:].bitcast(I32), in_=wl_words[0].bitcast(I32))
+        nc.sync.dma_start(list_b[:], offs2)
         for q in range(4):
-            load_scale_rows((nc.sync, nc.scalar, nc.sync, nc.gpsimd)[q], q, slice(0, 2), g_scales)
-        nc.gpsimd.dma_start(out=wl_raw[:].bitcast(I32), in_=wl_words[0].bitcast(I32))
-        make_identity(nc, ident[:])
-        for q in range(4):
-            load_scale_rows(nc.sync, q, slice(4, 5), wl_scales)
+            load_scale_rows(nc.sync, q, wl_sc_raw, wl_scales)
         gt_rows = gt.rearrange("(p r) t -> p r t", r=R)
 
         def load_gt(r):
@@ -80,26 +87,25 @@ def tile_list_merged_gradient_back_pl_kernel(
         wu_sb = sbt([P, 2, R, P], U32, "wu_sb")
         wu_sc = sbt([P, 2, R, P], U8, "wu_sc")
 
+        nc.vector.tensor_copy(out=wu_sc[:], in_=wu_sc_raw[:].rearrange("p z (q r) -> p z r q", r=R))
+
         def deal_wu(r0, r1):
             nc.vector.tensor_copy(
-                out=wu_sc[:, :, r0:r1, :].rearrange("p z r q -> p z q r"),
-                in_=scales_in[:, 2:4, :].rearrange("p z (q r) -> p z q r", r=R)[:, :, :, r0:r1],
-            )
-            nc.vector.tensor_copy(
-                out=wu_sb[:, :, r0:r1, :].bitcast(I32).rearrange("p z r q -> p z q r"),
-                in_=wu_raw[:].bitcast(I32).rearrange("p z (q r) -> p z q r", r=R)[:, :, :, r0:r1],
+                out=wu_sb[:, :, r0:r1, :].bitcast(I32).rearrange("p z r (c i) -> p z c r i", i=4),
+                in_=wu_raw[:].bitcast(I32).rearrange("p z (c i r) -> p z c r i", i=4, r=R)[:, :, :, r0:r1, :],
             )
 
         deal_wu(0, 1)
 
-        def first_product(acc, r, j0, width):
+        def first_product(acc, r, j0):
+            g_sb, c0 = (g_first, j0) if j0 < FIRST else (g_rest, j0 - FIRST)
             for z in range(2):
                 nc.tensor.matmul_mx(
                     out=acc,
                     lhsT=wu_sb[:, z, r, :].bitcast(E4M3X4),
                     lhsT_scale=wu_sc[:, z, r, :],
-                    rhs=g_sb[:, z, 2 * j0 : 2 * (j0 + width)].bitcast(E2M1X4),
-                    rhs_scale=scales_in[:, z, j0 : j0 + width],
+                    rhs=g_sb[:, z, 2 * c0 : 2 * (c0 + P)].bitcast(E2M1X4),
+                    rhs_scale=g_sc[:, z, j0 : j0 + P],
                     start=(z == 0),
                     stop=(z == 1),
                 )
@@ -110,9 +116,8 @@ def tile_list_merged_gradient_back_pl_kernel(
         def make_d(i):
             r, j0, j1 = pieces[i]
             acc = bank(i, [P, j1 - j0], "d_ps%d" % i)
-            step = HALF if j1 - j0 == HALF else P
-            for j in range(j0, j1, step):
-                first_product(acc[:, j - j0 : j - j0 + step], r, j, step)
+            for j in range(j0, j1, P):
+                first_product(acc[:, j - j0 : j - j0 + P], r, j)
             d_sb[i] = sbt([P, j1 - j0], F32, "d%d" % i)
             nc.scalar.activation(d_sb[i][:], acc[:], COPY, scale=0.5)
 
@@ -140,20 +145,19 @@ def tile_list_merged_gradient_back_pl_kernel(
         wl_sb = sbt([P, R, 2 * P], U8, "wl_sb")
         wl_sc = sbt([P, R, P], U8, "wl_sc")
 
-        pairs = [[sbt([P, 4, P, 2], BF16, "pairs%d%d" % (h, u)) for u in range(2)] for h in range(2)]
+        pairs = [[sbt([P, 2, P, 2], BF16, "pairs%d%d" % (h, q)) for q in range(2)] for h in range(2)]
         s_bf = [sbt([P, HALF, R], BF16, "s_bf%d" % h) for h in range(2)]
         back = [[bank(1 + 2 * h + q, [P, 2, 256], "back%d%d" % (h, q)) for q in range(2)] for h in range(2)]
 
         def turn_back(h, u):
-            words = pairs[h][u][:].rearrange("t b p e -> t b (p e)").bitcast(F32)
-            for tb in range(4):
-                c0 = (tb % 2) * P
-                nc.tensor.transpose(back[h][tb // 2][:, u, c0 : c0 + P], words[:, tb, :], ident[:])
-
-        def weave(h):
-            words = s_bf[h][:].rearrange("p t r -> p (t r)").bitcast(F32).rearrange("p (t u) -> p t u", u=2)
             for q in range(2):
-                nc.scalar.copy(words[:, 256 * q : 256 * (q + 1), :], back[h][q][:].rearrange("p u t -> p t u"))
+                words = pairs[h][q][:].rearrange("t b p e -> t b (p e)").bitcast(F32)
+                for tb in range(2):
+                    nc.tensor.transpose(back[h][q][:, u, tb * P : (tb + 1) * P], words[:, tb, :], ident[:])
+
+        def weave(h, q):
+            words = s_bf[h][:].rearrange("p t r -> p (t r)").bitcast(F32).rearrange("p (t u) -> p t u", u=2)
+            nc.scalar.copy(words[:, 256 * q : 256 * (q + 1), :], back[h][q][:].rearrange("p u t -> p t u"))
 
         gt_sb = {}
         for r in range(3):
@@ -163,12 +167,12 @@ def tile_list_merged_gradient_back_pl_kernel(
             scatter(page_b, list_b, r + 1)
             if r == 0:
                 nc.vector.tensor_copy(
-                    out=wl_sb[:].bitcast(U16).rearrange("p r q -> p q r"),
-                    in_=wl_raw[:].bitcast(U16).rearrange("p (q r) -> p q r", r=R),
+                    out=wl_sb[:].bitcast(U16),
+                    in_=wl_raw[:].bitcast(U16).rearrange("p (q r) -> p r q", r=R),
                 )
                 nc.vector.tensor_copy(
-                    out=wl_sc[:].rearrange("p r q -> p q r"),
-                    in_=scales_in[:, 4, :].rearrange("p (q r) -> p q r", r=R),
+                    out=wl_sc[:],
+                    in_=wl_sc_raw[:, 0, :].rearrange("p (q r) -> p r q", r=R),
                 )
             for h in range(2):
                 turn_add(sums[h], page_a, h * HALF, True, False)
@@ -177,72 +181,61 @@ def tile_list_merged_gradient_back_pl_kernel(
             for h in range(2):
                 turn_add(sums[h], page_b, h * HALF, False, True)
             for h in range(2):
-                if r == 2 and h == 0:
-                    nc.scalar.copy(pairs[0][1][:], sums[0][:].unsqueeze(3).to_broadcast([P, 4, P, 2]))
-                else:
-                    nc.scalar.copy(pairs[h][r // 2][:, :, :, r % 2], sums[h][:])
+                for q in range(2):
+                    nc.scalar.copy(pairs[h][q][:, :, :, r % 2], sums[h][:, 2 * q : 2 * q + 2, :])
             if r == 1:
                 turn_back(0, 0)
                 turn_back(1, 0)
-        turn_back(0, 1)
-        weave(0)
-
         gt_sb[3] = load_gt(3)
         scatter(page_a, list_a, 4)
-        part = bank(5, [P, 4, P], "part")
-        turn_add(part, gt_sb[3], 0, True, False)
-        turn_add(part, page_a, 0, False, True)
-        part_sb = sbt([P, 4, P], F32, "part_sb")
-        nc.scalar.copy(part_sb[:], part[:])
-        part_back = bank(6, [P, HALF], "part_back")
-        for tb in range(4):
-            nc.tensor.transpose(part_back[:, tb * P : (tb + 1) * P], part_sb[:, tb, :], ident[:])
-        last = [bank((5, 7)[q], [P, 2, P], "last%d" % q) for q in range(2)]
-        for q in range(2):
-            turn_add(last[q], gt_sb[3], HALF + 256 * q, True, False)
-            turn_add(last[q], page_a, HALF + 256 * q, False, False)
+        part_back = []
+        for h in range(2):
+            turn_back(h, 1)
+            weave(h, 0)
+            weave(h, 1)
+            part = bank(5 + h, [P, 4, P], "part%d" % h)
+            turn_add(part, gt_sb[3], h * HALF, True, False)
+            turn_add(part, page_a, h * HALF, False, True)
+            part_sb = sbt([P, 4, P], F32, "part_sb%d" % h)
+            nc.scalar.copy(part_sb[:], part[:])
+            part_back.append(bank(1 + 2 * h, [P, HALF], "part_back%d" % h))
+            for tb in range(4):
+                nc.tensor.transpose(part_back[h][:, tb * P : (tb + 1) * P], part_sb[:, tb, :], ident[:])
         scatter(page_b, list_b, 4)
-        for q in range(2):
-            turn_add(last[q], page_b, HALF + 256 * q, False, True)
 
         s_words = [sbt([P, HALF], U32, "s_words%d" % h) for h in range(2)]
         s_sc = [sbt([P, HALF], U8, "s_sc%d" % h) for h in range(2)]
-        for q in range(2):
-            cols = slice(256 * q, 256 * (q + 1))
-            nc.vector.tensor_tensor(s_bf[0][:, cols, 3], part_back[:, cols], page_b[:, cols], ADD)
-        for q in range(2):
-            cols = slice(256 * q, 256 * (q + 1))
-            nc.vector.quantize_mx(
-                out=s_words[0][:, cols].bitcast(E5M2X4), scales=s_sc[0][:, cols],
-                in_=s_bf[0][:, cols, :].rearrange("p t r -> p (t r)"),
-            )
-        for q in range(2):
-            nc.scalar.copy(pairs[1][1][:, 2 * q : 2 * q + 2, :, 1], last[q][:])
-        turn_back(1, 1)
-        weave(1)
+        for h in range(2):
+            for q in range(2):
+                cols = slice(256 * q, 256 * (q + 1))
+                page_cols = slice(h * HALF + 256 * q, h * HALF + 256 * (q + 1))
+                nc.vector.tensor_tensor(s_bf[h][:, cols, 3], part_back[h][:, cols], page_b[:, page_cols], ADD)
+            for q in range(2):
+                cols = slice(256 * q, 256 * (q + 1))
+                nc.vector.quantize_mx(
+                    out=s_words[h][:, cols].bitcast(E5M2X4), scales=s_sc[h][:, cols],
+                    in_=s_bf[h][:, cols, :].rearrange("p t r -> p (t r)"),
+                )
 
         y_rows = out_0.rearrange("(p r) t -> p r t", r=R)
         y_sb = [sbt([P, R, HALF], F32, "y_sb%d" % h) for h in range(2)]
         y_bf = [sbt([P, HALF, R], BF16, "y_bf%d" % h) for h in range(2)]
         y_words = sbt([P, T], U32, "y_words")
         y_sc = sbt([P, T], U8, "y_sc")
-        y_banks = [[5, 7, 5, 7], [6, 0, 1, 2]]
+        y_banks = [(7, 0, 2, 4), (5, 6, 1, 3)]
         words_out = out_1[0].rearrange("p t r -> p (t r)").bitcast(I32)
 
-        def second_product(h, r, on_vector):
+        def second_product(h, r):
             acc = bank(y_banks[h][r], [P, HALF], "y%d%d" % (h, r))
             nc.tensor.matmul_mx(
                 out=acc[:], lhsT=wl_sb[:, r, :].bitcast(E2M1X4), lhsT_scale=wl_sc[:, r, :],
                 rhs=s_words[h][:].bitcast(E5M2X4), rhs_scale=s_sc[h][:], start=True, stop=True,
             )
-            if on_vector:
-                nc.vector.tensor_copy(y_sb[h][:, r, :], acc[:])
-            else:
-                nc.scalar.copy(y_sb[h][:, r, :], acc[:])
+            nc.scalar.copy(y_sb[h][:, r, :], acc[:])
             nc.sync.dma_start(out=y_rows[:, r, h * HALF : (h + 1) * HALF], in_=y_sb[h][:, r, :])
 
-        def planes(h, t0, t1):
-            nc.vector.tensor_copy(
+        def planes(h, t0, t1, copy):
+            copy(
                 out=y_bf[h][:, t0:t1, :].rearrange("p (c i) r -> p c r i", i=4),
                 in_=y_sb[h][:, :, t0:t1].rearrange("p r (c i) -> p c r i", i=4),
             )
@@ -254,22 +247,20 @@ def tile_list_merged_gradient_back_pl_kernel(
                 in_=y_bf[h][:, t0:t1, :].rearrange("p t r -> p (t r)"),
             )
 
-        second_product(0, 0, True)
-        second_product(0, 1, False)
-        nc.vector.quantize_mx(
-            out=s_words[1][:].bitcast(E5M2X4), scales=s_sc[1][:], in_=s_bf[1][:].rearrange("p t r -> p (t r)")
-        )
-        second_product(0, 2, True)
-        second_product(0, 3, False)
-        for r in range(R):
-            second_product(1, r, False)
         for h in range(2):
-            planes(h, 0, 256)
-            planes(h, 256, 512)
+            for r in range(R):
+                second_product(h, r)
+        for h in range(2):
+            planes(h, 0, 256, nc.vector.tensor_copy)
+            if h == 0:
+                planes(h, 256, 512, nc.vector.tensor_copy)
+            else:
+                planes(h, 384, 512, nc.scalar.copy)
+                planes(h, 256, 384, nc.vector.tensor_copy)
             for q in range(2):
                 planes_q(h, 256 * q, 256 * (q + 1))
-                cols = slice(h * HALF + 256 * q, h * HALF + 256 * (q + 1))
-                nc.sync.dma_start(out=words_out[:, cols], in_=y_words[:, cols].bitcast(I32))
+            cols = slice(h * HALF, (h + 1) * HALF)
+            nc.sync.dma_start(out=words_out[:, cols], in_=y_words[:, cols].bitcast(I32))
         for q in range(4):
             queue = nc.sync if q % 2 == 0 else nc.scalar
             queue.dma_start(

@@ -155,9 +155,10 @@ def tile_list_merged_gradient_back_pl_kernel(
                 for tb in range(2):
                     nc.tensor.transpose(back[h][q][:, u, tb * P : (tb + 1) * P], words[:, tb, :], ident[:])
 
-        def weave(h, q):
-            words = s_bf[h][:].rearrange("p t r -> p (t r)").bitcast(F32).rearrange("p (t u) -> p t u", u=2)
-            nc.scalar.copy(words[:, 256 * q : 256 * (q + 1), :], back[h][q][:].rearrange("p u t -> p t u"))
+        word_rows = [sbt([P, 2, HALF], F32, "word_rows%d" % h) for h in range(2)]
+
+        def unload(h, q):
+            nc.scalar.copy(word_rows[h][:, :, 256 * q : 256 * (q + 1)], back[h][q][:])
 
         gt_sb = {}
         for r in range(3):
@@ -191,8 +192,8 @@ def tile_list_merged_gradient_back_pl_kernel(
         part_back = []
         for h in range(2):
             turn_back(h, 1)
-            weave(h, 0)
-            weave(h, 1)
+            unload(h, 0)
+            unload(h, 1)
             part = bank(5 + h, [P, 4, P], "part%d" % h)
             turn_add(part, gt_sb[3], h * HALF, True, False)
             turn_add(part, page_a, h * HALF, False, True)
@@ -209,7 +210,12 @@ def tile_list_merged_gradient_back_pl_kernel(
             for q in range(2):
                 cols = slice(256 * q, 256 * (q + 1))
                 page_cols = slice(h * HALF + 256 * q, h * HALF + 256 * (q + 1))
-                nc.vector.tensor_tensor(s_bf[h][:, cols, 3], part_back[h][:, cols], page_b[:, page_cols], ADD)
+                halves = word_rows[h][:, 1, cols].bitcast(BF16).rearrange("p (t e) -> p t e", e=2)
+                nc.vector.tensor_tensor(halves[:, :, 1], part_back[h][:, cols], page_b[:, page_cols], ADD)
+            words = s_bf[h][:].rearrange("p t r -> p (t r)").bitcast(F32).rearrange("p (t u) -> p t u", u=2)
+            for q in range(2):
+                cols = slice(256 * q, 256 * (q + 1))
+                nc.vector.tensor_copy(words[:, cols, :], word_rows[h][:, :, cols].rearrange("p u t -> p t u"))
             for q in range(2):
                 cols = slice(256 * q, 256 * (q + 1))
                 nc.vector.quantize_mx(
@@ -231,7 +237,8 @@ def tile_list_merged_gradient_back_pl_kernel(
                 out=acc[:], lhsT=wl_sb[:, r, :].bitcast(E2M1X4), lhsT_scale=wl_sc[:, r, :],
                 rhs=s_words[h][:].bitcast(E5M2X4), rhs_scale=s_sc[h][:], start=True, stop=True,
             )
-            nc.scalar.copy(y_sb[h][:, r, :], acc[:])
+            copy = nc.vector.tensor_copy if (h, r) == (1, 0) else nc.scalar.copy
+            copy(y_sb[h][:, r, :], acc[:])
             nc.sync.dma_start(out=y_rows[:, r, h * HALF : (h + 1) * HALF], in_=y_sb[h][:, r, :])
 
         def planes(h, t0, t1, copy):

@@ -70,9 +70,9 @@ def tile_list_merged_gradient_back_pl_kernel(
             load_scale_rows(nc.sync if q < 2 else nc.scalar, q, wu_sc_raw, wu_scales)
         nc.sync.dma_start(out=wu_raw[:].bitcast(I32), in_=wu_words.rearrange("z p c r -> p z (c r)").bitcast(I32))
         for q in range(4):
-            load_scale_rows(nc.sync if q < 1 else nc.scalar, q, g_sc, g_scales)
+            load_scale_rows((nc.sync, nc.scalar, nc.scalar, nc.gpsimd)[q], q, g_sc, g_scales)
         nc.sync.dma_start(list_a[:], offs)
-        nc.scalar.dma_start(out=g_rest[:].bitcast(I32), in_=g_rows[:, :, 2 * FIRST : 2 * J].bitcast(I32))
+        nc.sync.dma_start(out=g_rest[:].bitcast(I32), in_=g_rows[:, :, 2 * FIRST : 2 * J].bitcast(I32))
         nc.sync.dma_start(out=wl_raw[:].bitcast(I32), in_=wl_words[0].bitcast(I32))
         nc.sync.dma_start(list_b[:], offs2)
         for q in range(4):

from contextlib import ExitStack

import concourse.mybir as mybir
from concourse.masks import make_identity

N, M, K, T, J = 1024, 512, 512, 1024, 512
FLOPS = 2 * N * M * J + 2 * M * K * T

F32 = mybir.dt.float32
BF16 = mybir.dt.bfloat16
I32 = mybir.dt.int32
U32 = mybir.dt.uint32
U16 = mybir.dt.uint16
U8 = mybir.dt.uint8
E4M3X4 = mybir.dt.float8_e4m3fn_x4
E5M2X4 = mybir.dt.float8_e5m2_x4
E2M1X4 = mybir.dt.float4_e2m1fn_x4
COPY = mybir.ActivationFunctionType.Copy
ADD = mybir.AluOpType.add

P = 128
R = 4
HALF = 512
FIRST = 128


def tile_list_merged_gradient_back_pl_kernel(
    tc, g_words, g_scales, wu_words, wu_scales, gt, wl_words, wl_scales, offs, offs2, out_0, out_1, out_2
):
    nc = tc.nc
    with ExitStack() as ctx:
        sb = ctx.enter_context(tc.tile_pool(name="sb", bufs=1))
        ps = ctx.enter_context(tc.psum_pool(name="ps", bufs=1))

        def bank(b, shape, name):
            return ps.tile(shape, F32, name=name, tag="bank%d" % b)

        def sbt(shape, dtype, name):
            return sb.tile(shape, dtype, name=name, align_bytes=64)

        list_a = sb.tile([P, J // 16], U16, name="list_a")
        list_b = sb.tile([P, J // 16], U16, name="list_b")
        wu_sc_raw = sbt([P, 2, M], U8, "wu_sc_raw")
        g_sc = sbt([P, 2, J], U8, "g_sc")
        wl_sc_raw = sbt([P, 1, K], U8, "wl_sc_raw")
        wu_raw = sb.tile([P, 2, M], U32, name="wu_raw", tag="stage", align_bytes=64)
        g_first = sbt([P, 2, 2 * FIRST], U8, "g_first")
        g_rest = sbt([P, 2, 2 * (J - FIRST)], U8, "g_rest")
        wl_raw = sbt([P, 2 * K], U8, "wl_raw")
        page_a = sbt([P, T], F32, "page_a")
        page_b = sbt([P, T], F32, "page_b")
        ident = sbt([P, P], F32, "ident")

        for plane in (wu_sc_raw, g_sc, wl_sc_raw):
            nc.vector.memset(plane[:].rearrange("p a c -> p (a c)").bitcast(I32), 0)
        nc.vector.memset(page_a[:], 0.0)
        nc.vector.memset(page_b[:], 0.0)
        nc.vector.memset(ident[:], 0.0)
        make_identity(nc, ident[:], nomemset=True)

        def load_scale_rows(queue, q, plane, src):
            queue.dma_start(
                out=plane[32 * q : 32 * q + 4].bitcast(I32),
                in_=src[:, 4 * q : 4 * q + 4, :].rearrange("z q c -> q z c").bitcast(I32),
            )

        g_rows = g_words.rearrange("z p c -> p z c")
        nc.sync.dma_start(out=g_first[:].bitcast(I32), in_=g_rows[:, :, 0 : 2 * FIRST].bitcast(I32))
        for q in range(4):
            load_scale_rows(nc.sync if q < 2 else nc.scalar, q, wu_sc_raw, wu_scales)
        nc.sync.dma_start(out=wu_raw[:].bitcast(I32), in_=wu_words.rearrange("z p c r -> p z (c r)").bitcast(I32))
        for q in range(4):
            load_scale_rows((nc.sync, nc.scalar, nc.scalar, nc.gpsimd)[q], q, g_sc, g_scales)
        nc.sync.dma_start(list_a[:], offs)
        nc.sync.dma_start(out=g_rest[:].bitcast(I32), in_=g_rows[:, :, 2 * FIRST : 2 * J].bitcast(I32))
        nc.sync.dma_start(out=wl_raw[:].bitcast(I32), in_=wl_words[0].bitcast(I32))
        nc.sync.dma_start(list_b[:], offs2)
        for q in range(4):
            load_scale_rows(nc.sync, q, wl_sc_raw, wl_scales)
        gt_rows = gt.rearrange("(p r) t -> p r t", r=R)

        def load_gt(r):
            tile = sb.tile([P, T], F32, name="gt%d" % r, tag="stage", align_bytes=64)
            nc.sync.dma_start(out=tile[:], in_=gt_rows[:, r, :])
            return tile

        wu_sb = sbt([P, 2, R, P], U32, "wu_sb")
        wu_sc = sbt([P, 2, R, P], U8, "wu_sc")

        nc.vector.tensor_copy(out=wu_sc[:], in_=wu_sc_raw[:].rearrange("p z (q r) -> p z r q", r=R))

        def deal_wu(r0, r1):
            nc.vector.tensor_copy(
                out=wu_sb[:, :, r0:r1, :].bitcast(I32).rearrange("p z r (c i) -> p z c r i", i=4),
                in_=wu_raw[:].bitcast(I32).rearrange("p z (c i r) -> p z c r i", i=4, r=R)[:, :, :, r0:r1, :],
            )

        deal_wu(0, 1)

        def first_product(acc, r, j0):
            g_sb, c0 = (g_first, j0) if j0 < FIRST else (g_rest, j0 - FIRST)
            for z in range(2):
                nc.tensor.matmul_mx(
                    out=acc,
                    lhsT=wu_sb[:, z, r, :].bitcast(E4M3X4),
                    lhsT_scale=wu_sc[:, z, r, :],
                    rhs=g_sb[:, z, 2 * c0 : 2 * (c0 + P)].bitcast(E2M1X4),
                    rhs_scale=g_sc[:, z, j0 : j0 + P],
                    start=(z == 0),
                    stop=(z == 1),
                )

        pieces = [(0, 0, FIRST), (0, FIRST, J), (1, 0, J), (2, 0, J), (3, 0, J)]
        d_sb = {}

        def make_d(i):
            r, j0, j1 = pieces[i]
            acc = bank(i, [P, j1 - j0], "d_ps%d" % i)
            for j in range(j0, j1, P):
                first_product(acc[:, j - j0 : j - j0 + P], r, j)
            d_sb[i] = sbt([P, j1 - j0], F32, "d%d" % i)
            nc.scalar.activation(d_sb[i][:], acc[:], COPY, scale=0.5)

        def scatter(page, lst, i):
            r, j0, j1 = pieces[i]
            nc.vector.tensor_copy(page[:].indirect(lst[:, j0 // 16 : j1 // 16]), d_sb[i][:])

        make_d(0)
        make_d(1)
        scatter(page_a, list_a, 0)
        scatter(page_b, list_b, 0)
        deal_wu(1, R)
        for i in range(2, len(pieces)):
            make_d(i)

        def turn_add(acc, src, t0, start, stop):
            blocks = acc.shape[1]
            for tb in range(blocks):
                c0 = t0 + tb * P
                nc.tensor.matmul(
                    acc[:, tb, :], lhsT=src[:, c0 : c0 + P], rhs=ident[:], is_transpose=True,
                    start=(start and tb == 0), stop=(stop and tb == blocks - 1),
                )

        wl_sb = sbt([P, R, 2 * P], U8, "wl_sb")
        wl_sc = sbt([P, R, P], U8, "wl_sc")

        pairs = [[sbt([P, 2, P, 2], BF16, "pairs%d%d" % (h, q)) for q in range(2)] for h in range(2)]
        s_bf = [sbt([P, HALF, R], BF16, "s_bf%d" % h) for h in range(2)]
        back = [[bank(1 + 2 * h + q, [P, 2, 256], "back%d%d" % (h, q)) for q in range(2)] for h in range(2)]

        def turn_back(h, u):
            for q in range(2):
                words = pairs[h][q][:].rearrange("t b p e -> t b (p e)").bitcast(F32)
                for tb in range(2):
                    nc.tensor.transpose(back[h][q][:, u, tb * P : (tb + 1) * P], words[:, tb, :], ident[:])

        word_rows = [sbt([P, 2, HALF], F32, "word_rows%d" % h) for h in range(2)]

        def unload(h, q):
            nc.scalar.copy(word_rows[h][:, :, 256 * q : 256 * (q + 1)], back[h][q][:])

        gt_sb = {}
        for r in range(3):
            gt_sb[r] = load_gt(r)
            sums = [bank(5 + h, [P, 4, P], "sum%d%d" % (r, h)) for h in range(2)]
            scatter(page_a, list_a, r + 1)
            scatter(page_b, list_b, r + 1)
            if r == 0:
                nc.vector.tensor_copy(
                    out=wl_sb[:].bitcast(U16),
                    in_=wl_raw[:].bitcast(U16).rearrange("p (q r) -> p r q", r=R),
                )
                nc.vector.tensor_copy(
                    out=wl_sc[:],
                    in_=wl_sc_raw[:, 0, :].rearrange("p (q r) -> p r q", r=R),
                )
            for h in range(2):
                turn_add(sums[h], page_a, h * HALF, True, False)
            for h in range(2):
                turn_add(sums[h], gt_sb[r], h * HALF, False, False)
            for h in range(2):
                turn_add(sums[h], page_b, h * HALF, False, True)
            for h in range(2):
                for q in range(2):
                    nc.scalar.copy(pairs[h][q][:, :, :, r % 2], sums[h][:, 2 * q : 2 * q + 2, :])
            if r == 1:
                turn_back(0, 0)
                turn_back(1, 0)
        gt_sb[3] = load_gt(3)
        scatter(page_a, list_a, 4)
        part_back = []
        for h in range(2):
            turn_back(h, 1)
            unload(h, 0)
            unload(h, 1)
            part = bank(5 + h, [P, 4, P], "part%d" % h)
            turn_add(part, gt_sb[3], h * HALF, True, False)
            turn_add(part, page_a, h * HALF, False, True)
            part_sb = sbt([P, 4, P], F32, "part_sb%d" % h)
            nc.scalar.copy(part_sb[:], part[:])
            part_back.append(bank(1 + 2 * h, [P, HALF], "part_back%d" % h))
            for tb in range(4):
                nc.tensor.transpose(part_back[h][:, tb * P : (tb + 1) * P], part_sb[:, tb, :], ident[:])
        scatter(page_b, list_b, 4)

        s_words = [sbt([P, HALF], U32, "s_words%d" % h) for h in range(2)]
        s_sc = [sbt([P, HALF], U8, "s_sc%d" % h) for h in range(2)]
        for h in range(2):
            for q in range(2):
                cols = slice(256 * q, 256 * (q + 1))
                page_cols = slice(h * HALF + 256 * q, h * HALF + 256 * (q + 1))
                halves = word_rows[h][:, 1, cols].bitcast(BF16).rearrange("p (t e) -> p t e", e=2)
                nc.vector.tensor_tensor(halves[:, :, 1], part_back[h][:, cols], page_b[:, page_cols], ADD)
            words = s_bf[h][:].rearrange("p t r -> p (t r)").bitcast(F32).rearrange("p (t u) -> p t u", u=2)
            for q in range(2):
                cols = slice(256 * q, 256 * (q + 1))
                nc.vector.tensor_copy(words[:, cols, :], word_rows[h][:, :, cols].rearrange("p u t -> p t u"))
            for q in range(2):
                cols = slice(256 * q, 256 * (q + 1))
                nc.vector.quantize_mx(
                    out=s_words[h][:, cols].bitcast(E5M2X4), scales=s_sc[h][:, cols],
                    in_=s_bf[h][:, cols, :].rearrange("p t r -> p (t r)"),
                )

        y_rows = out_0.rearrange("(p r) t -> p r t", r=R)
        y_sb = [sbt([P, R, HALF], F32, "y_sb%d" % h) for h in range(2)]
        y_bf = [sbt([P, HALF, R], BF16, "y_bf%d" % h) for h in range(2)]
        y_words = sbt([P, T], U32, "y_words")
        y_sc = sbt([P, T], U8, "y_sc")
        y_banks = [(7, 0, 2, 4), (5, 6, 1, 3)]
        words_out = out_1[0].rearrange("p t r -> p (t r)").bitcast(I32)

        def second_product(h, r):
            acc = bank(y_banks[h][r], [P, HALF], "y%d%d" % (h, r))
            nc.tensor.matmul_mx(
                out=acc[:], lhsT=wl_sb[:, r, :].bitcast(E2M1X4), lhsT_scale=wl_sc[:, r, :],
                rhs=s_words[h][:].bitcast(E5M2X4), rhs_scale=s_sc[h][:], start=True, stop=True,
            )
            copy = nc.vector.tensor_copy if (h, r) == (1, 0) else nc.scalar.copy
            copy(y_sb[h][:, r, :], acc[:])
            nc.sync.dma_start(out=y_rows[:, r, h * HALF : (h + 1) * HALF], in_=y_sb[h][:, r, :])

        def planes(h, t0, t1, copy):
            copy(
                out=y_bf[h][:, t0:t1, :].rearrange("p (c i) r -> p c r i", i=4),
                in_=y_sb[h][:, :, t0:t1].rearrange("p r (c i) -> p c r i", i=4),
            )

        def planes_q(h, t0, t1):
            cols = slice(h * HALF + t0, h * HALF + t1)
            nc.vector.quantize_mx(
                out=y_words[:, cols].bitcast(E4M3X4), scales=y_sc[:, cols],
                in_=y_bf[h][:, t0:t1, :].rearrange("p t r -> p (t r)"),
            )

        for h in range(2):
            for r in range(R):
                second_product(h, r)
        for h in range(2):
            planes(h, 0, 256, nc.vector.tensor_copy)
            if h == 0:
                planes(h, 256, 512, nc.vector.tensor_copy)
            else:
                planes(h, 384, 512, nc.scalar.copy)
                planes(h, 256, 384, nc.vector.tensor_copy)
            for q in range(2):
                planes_q(h, 256 * q, 256 * (q + 1))
            cols = slice(h * HALF, (h + 1) * HALF)
            nc.sync.dma_start(out=words_out[:, cols], in_=y_words[:, cols].bitcast(I32))
        for q in range(4):
            queue = nc.sync if q % 2 == 0 else nc.scalar
            queue.dma_start(
                out=out_2[0, 4 * q : 4 * q + 4, :].bitcast(I32), in_=y_sc[32 * q : 32 * q + 4, :].bitcast(I32)
            )
